import numpy as np
import ml_dtypes


def mxq(x, axis, fmt="e4m3"):
    dtype, down = {"e4m3": (ml_dtypes.float8_e4m3fn, 7), "e5m2": (ml_dtypes.float8_e5m2, 14)}[fmt]
    v = np.moveaxis(np.asarray(x, np.float32).astype(ml_dtypes.bfloat16).astype(np.float64), axis, -1)
    blocks = v.reshape(v.shape[:-1] + (-1, 32))
    amax = np.abs(blocks).max(-1, keepdims=True)
    byte = np.maximum(np.where(amax > 0, np.frexp(amax)[1] - 1 + 127, 0) - down, 1)
    scale = np.exp2(byte - 127.0)
    codes = (blocks / scale).astype(np.float32).astype(dtype).astype(np.float64)
    return np.moveaxis((codes * scale).reshape(v.shape), -1, axis)


WIDE = False


def mx_kscale(k):
    if not WIDE:
        return np.ones(k)
    levels = np.array([10, -10, 5, -5, 0])
    if k % 512:
        return np.exp2(np.random.permutation(np.resize(levels, k // 32))).repeat(32)
    a = np.empty((k // 512, 16))
    for p in range(k // 512):
        a[p, :8] = np.random.permutation(np.resize(levels, 8))
        for g in range(8):
            far = levels[np.abs(levels - a[p, g]) >= 10]
            a[p, g + 8] = far[np.random.randint(len(far))]
    return np.exp2(a.ravel()).repeat(32)


def f64(x):
    return np.asarray(x).astype(np.float64)


def striped(idx):
    return np.tile(idx.reshape(-1, 16).T, (8, 1)).astype(np.uint16)


def unstriped(offs):
    return offs[:16].T.reshape(-1).astype(np.int64)


def pack_weight(w):
    k, n = w.shape
    w = f64(np.asarray(w, np.float32).astype(ml_dtypes.bfloat16)).reshape(k // 32, 32, n)
    amax = np.abs(w).max(1)
    byte = np.clip(np.where(amax > 0, np.frexp(amax)[1] - 1 + 127 - 7, 1), 1, 254)
    scaled = (w * np.exp2(127.0 - byte)[:, None, :]).reshape(k, n).astype(np.float32)
    words = np.ascontiguousarray(scaled.reshape(k // 512, 128, 4, n).transpose(0, 1, 3, 2)).astype(ml_dtypes.float8_e4m3fn).view(np.uint8)
    return words, np.ascontiguousarray(byte.astype(np.uint8).reshape(k // 512, 16, n))


def unpack_weight(words, scales):
    g, p, n, _ = words.shape
    vals = np.ascontiguousarray(words).view(ml_dtypes.float8_e4m3fn).astype(np.float64) * np.repeat(np.exp2(scales.astype(np.float64) - 127.0), 8, axis=1)[..., None]
    return vals.transpose(0, 1, 3, 2).reshape(g * 512, n)


K, T, E, C, N = 512, 512, 4, 256, 512


def by_expert(wq, xq):
    return np.concatenate([wq[e].T @ xq[:, e * C:(e + 1) * C] for e in range(E)], axis=1)


def setup_inputs():
    n = np.random.standard_normal
    s = mx_kscale(K)[:, None]
    first = np.random.permutation(np.repeat(np.arange(E), T // E))
    second = (first + 1 + np.random.permutation(np.repeat(np.arange(E - 1), -(-T // (E - 1)))[:T])) % E
    while np.bincount(second, minlength=E).max() != T // E:
        load = np.bincount(second, minlength=E); hi, lo = int(load.argmax()), int(load.argmin())
        t = np.flatnonzero((second == hi) & (first != lo))[0]; second[t] = lo
    slot_token = np.empty(E * C, np.int64); pos = np.empty((2, T), np.int64); fill = np.zeros(E, np.int64)
    place = np.stack([np.random.permutation(C) for _ in range(E)])
    for r, deal in enumerate((first, second)):
        for t in np.random.permutation(T):
            e = deal[t]; j = e * C + place[e, fill[e]]; fill[e] += 1; slot_token[j] = t; pos[r, t] = j
    g = np.random.uniform(0.2, 0.8, T)
    packed = [pack_weight(m) for m in n((E, K, N)) / np.sqrt(K) / s[None]]
    return {
        "xT": (n((K, T)) * s).astype(np.float32),
        "w_words": np.stack([m[0] for m in packed]),
        "w_scales": np.stack([m[1] for m in packed]),
        "gate": np.stack([np.tile(g, (N, 1)), np.tile(1.0 - g, (N, 1))]).astype(np.float32),
        "offs": striped(slot_token),
        "pos1": striped(pos[0]),
        "pos2": striped(pos[1]),
    }


def reference(xT, w_words, w_scales, gate, offs, pos1, pos2):
    idx = unstriped(offs)
    xq = mxq(f64(xT)[:, idx], 0, "e4m3")
    w = np.stack([unpack_weight(w_words[e], w_scales[e]) for e in range(E)])
    y = by_expert(w, xq)
    return f64(gate[0]) * y[:, unstriped(pos1)] + f64(gate[1]) * y[:, unstriped(pos2)]

@@ -1,0 +1,136 @@
+from contextlib import ExitStack
+
+import concourse.mybir as mybir
+
+K, T, E, C, N = 512, 512, 4, 256, 512
+P = 128
+SLOTS = E * C
+BLOCKS = N // P
+FLOPS = 2 * K * N * SLOTS
+BYTES = 4 * K * T + E * K * N + E * K * N // 32 + 4 * 2 * T + 2 * P * (SLOTS + 2 * T) // 16 + 4 * N * T
+
+F32 = mybir.dt.float32
+BF16 = mybir.dt.bfloat16
+U32 = mybir.dt.uint32
+I32 = mybir.dt.int32
+U16 = mybir.dt.uint16
+U8 = mybir.dt.uint8
+FP8X4 = mybir.dt.float8_e4m3fn_x4
+mult = mybir.AluOpType.mult
+add = mybir.AluOpType.add
+
+HALF = T // 2
+V_COLS = 160
+
+
+def tile_routed_moe_kernel(tc, xT, w_words, w_scales, gate, offs, pos1, pos2, out):
+    nc = tc.nc
+    with ExitStack() as ctx:
+        keep = ctx.enter_context(tc.tile_pool(name="keep", bufs=1))
+        psum = ctx.enter_context(tc.psum_pool(name="psum", bufs=1))
+
+        x_raw = [keep.tile([P, 4, HALF], F32, name=f"x_raw{h}") for h in range(2)]
+        x_view = xT.rearrange("(p t) n -> p t n", t=4)
+        nc.sync.dma_start(out=x_raw[0][:], in_=x_view[:, :, 0:HALF])
+        nc.scalar.dma_start(out=x_raw[1][:], in_=x_view[:, :, HALF:T])
+
+        offs_t = keep.tile([P, SLOTS // 16], U16, name="offs_t")
+        nc.sync.dma_start(offs_t[:], offs)
+
+        w_t = keep.tile([P, E, N], U32, name="w_t", align_bytes=64)
+        w_sc = keep.tile([P, N], U8, name="w_sc", align_bytes=64)
+        nc.gpsimd.memset(w_sc[:], 0)
+        x_sc = keep.tile([P, T], U8, name="x_sc", align_bytes=64)
+        nc.gpsimd.memset(x_sc[:], 0)
+        for q in range(4):
+            nc.sync.dma_start(
+                out=w_sc[32 * q : 32 * q + 16, :].bitcast(I32),
+                in_=w_scales[:, 0, 4 * q : 4 * q + 4, :].bitcast(I32),
+            )
+        w_view = w_words.rearrange("e a p n r -> p (e a) (n r)").bitcast(I32)
+        nc.sync.dma_start(out=w_t[:, 0:2, :].bitcast(I32), in_=w_view[:, 0:2, :])
+        nc.sync.dma_start(out=w_t[:, 2:4, :].bitcast(I32), in_=w_view[:, 2:4, :])
+        pos_t = [keep.tile([P, T // 16], U16, name=f"pos_t{r}") for r in range(2)]
+        nc.sync.dma_start(pos_t[0][:], pos1)
+        nc.sync.dma_start(pos_t[1][:], pos2)
+        gate_t = keep.tile([P, 2, T], F32, name="gate_t")
+        nc.sync.dma_start(out=gate_t[:], in_=gate[:, 0:P, :].rearrange("g p t -> p g t"))
+
+        x_codes = keep.tile([P, T], U32, name="x_codes", align_bytes=64)
+        for h in range(2):
+            x_bf = keep.tile([P, HALF, 4], BF16, name=f"x_bf{h}", align_bytes=64)
+            src = x_raw[h][:].rearrange("p t n -> p n t")
+            nc.vector.tensor_copy(out=x_bf[:, 0:V_COLS, :], in_=src[:, 0:V_COLS, :])
+            nc.scalar.copy(out=x_bf[:, V_COLS:HALF, :], in_=src[:, V_COLS:HALF, :])
+            cols = slice(h * HALF, (h + 1) * HALF)
+            nc.vector.quantize_mx(
+                out=x_codes[:, cols].bitcast(FP8X4),
+                scales=x_sc[:, cols],
+                in_=x_bf[:].rearrange("p n t -> p (n t)"),
+            )
+
+        s_codes = keep.tile([P, SLOTS], U32, name="s_codes", align_bytes=64)
+        s_sc = keep.tile([P, SLOTS], U8, name="s_sc", align_bytes=64)
+        banks = [[psum.tile([P, 2 * C], F32, name=f"bank{b}_{h}") for h in range(2)] for b in range(BLOCKS)]
+        y = [keep.tile([P, SLOTS], F32, name=f"y{b}") for b in range(BLOCKS)]
+
+        def gather(a, z):
+            o = offs_t[:, a // 16 : z // 16]
+            nc.vector.tensor_copy(s_codes[:, a:z], x_codes[:].indirect(o))
+            nc.vector.tensor_copy(s_sc[:, a:z], x_sc[:].indirect(o))
+
+        def multiply(b, a, z):
+            e = a // C
+            cols = slice(b * P, (b + 1) * P)
+            h, off = divmod(a, 2 * C)
+            nc.tensor.matmul_mx(
+                out=banks[b][h][:, off : off + z - a],
+                lhsT=w_t[:, e, cols].bitcast(FP8X4),
+                lhsT_scale=w_sc[4 * e : P, cols],
+                rhs=s_codes[:, a:z].bitcast(FP8X4),
+                rhs_scale=s_sc[:, a:z],
+                start=True,
+                stop=True,
+            )
+
+        gather(0, 384)
+        for b in range(BLOCKS):
+            multiply(b, 0, 256)
+            multiply(b, 256, 384)
+        gather(384, 768)
+        for b in range(BLOCKS):
+            multiply(b, 384, 512)
+            multiply(b, 512, 768)
+        nc.scalar.copy(out=y[0][:, 0:512], in_=banks[0][0][:])
+        nc.scalar.copy(out=y[0][:, 512:768], in_=banks[0][1][:, 0:256])
+        gather(768, 1024)
+        for b in range(BLOCKS):
+            multiply(b, 768, 1024)
+        nc.vector.tensor_copy(out=y[0][:, 768:1024], in_=banks[0][1][:, 256:512])
+        for b in range(1, BLOCKS):
+            nc.scalar.copy(out=y[b][:, 0:512], in_=banks[b][0][:])
+            nc.scalar.copy(out=y[b][:, 512:1024], in_=banks[b][1][:])
+
+        z = [[keep.tile([P, T], F32, name=f"z{b}_{r}") for r in range(2)] for b in range(BLOCKS)]
+        o_t = [keep.tile([P, T], F32, name=f"o{b}") for b in range(BLOCKS)]
+
+        def fetch(b, r, c0=0, c1=T):
+            o = pos_t[r][:] if (c0, c1) == (0, T) else pos_t[r][:, c0 // 16 : c1 // 16]
+            nc.vector.tensor_tensor(z[b][r][:, c0:c1], y[b][:].indirect(o), gate_t[:, r, c0:c1], mult)
+
+        def finish(b, c0=0, c1=T):
+            nc.vector.tensor_tensor(o_t[b][:, c0:c1], z[b][0][:, c0:c1], z[b][1][:, c0:c1], add)
+            nc.sync.dma_start(out=out[b * P : (b + 1) * P, c0:c1], in_=o_t[b][:, c0:c1])
+
+        fetch(0, 0)
+        fetch(0, 1)
+        for b in range(1, BLOCKS):
+            fetch(b, 0)
+            finish(b - 1)
+            if b < BLOCKS - 1:
+                fetch(b, 1)
+        b = BLOCKS - 1
+        fetch(b, 1, 0, 256)
+        fetch(b, 1, 256, 512)
+        finish(b, 0, 256)
+        finish(b, 256, 512)

@@ -1,6 +1,7 @@
 from contextlib import ExitStack
 
 import concourse.mybir as mybir
+from concourse.masks import make_identity
 
 K, T, E, C, N = 512, 512, 4, 256, 512
 P = 128
@@ -17,10 +18,10 @@ U16 = mybir.dt.uint16
 U8 = mybir.dt.uint8
 FP8X4 = mybir.dt.float8_e4m3fn_x4
 mult = mybir.AluOpType.mult
+COPY = mybir.ActivationFunctionType.Copy
 add = mybir.AluOpType.add
 
-HALF = T // 2
-V_COLS = 160
+V_COLS = 352
 
 
 def tile_routed_moe_kernel(tc, xT, w_words, w_scales, gate, offs, pos1, pos2, out):
@@ -29,19 +30,18 @@ def tile_routed_moe_kernel(tc, xT, w_words, w_scales, gate, offs, pos1, pos2, ou
         keep = ctx.enter_context(tc.tile_pool(name="keep", bufs=1))
         psum = ctx.enter_context(tc.psum_pool(name="psum", bufs=1))
 
-        x_raw = [keep.tile([P, 4, HALF], F32, name=f"x_raw{h}") for h in range(2)]
-        x_view = xT.rearrange("(p t) n -> p t n", t=4)
-        nc.sync.dma_start(out=x_raw[0][:], in_=x_view[:, :, 0:HALF])
-        nc.scalar.dma_start(out=x_raw[1][:], in_=x_view[:, :, HALF:T])
-
+        x_raw = [keep.tile([P, 2, T], F32, name=f"x_raw{u}") for u in range(2)]
+        x_view = xT.rearrange("(p u r) n -> u p r n", u=2, r=2)
+        nc.sync.dma_start(out=x_raw[0][:, :, 0:V_COLS], in_=x_view[0][:, :, 0:V_COLS])
+        nc.scalar.dma_start(out=x_raw[0][:, :, V_COLS:T], in_=x_view[0][:, :, V_COLS:T])
         offs_t = keep.tile([P, SLOTS // 16], U16, name="offs_t")
         nc.sync.dma_start(offs_t[:], offs)
+        for r in range(2):
+            nc.sync.dma_start(out=x_raw[1][:, r, :], in_=x_view[1][:, r, :])
 
         w_t = keep.tile([P, E, N], U32, name="w_t", align_bytes=64)
         w_sc = keep.tile([P, N], U8, name="w_sc", align_bytes=64)
-        nc.gpsimd.memset(w_sc[:], 0)
-        x_sc = keep.tile([P, T], U8, name="x_sc", align_bytes=64)
-        nc.gpsimd.memset(x_sc[:], 0)
+        nc.vector.memset(w_sc[:].bitcast(I32), 0)
         for q in range(4):
             nc.sync.dma_start(
                 out=w_sc[32 * q : 32 * q + 16, :].bitcast(I32),
@@ -56,35 +56,47 @@ def tile_routed_moe_kernel(tc, xT, w_words, w_scales, gate, offs, pos1, pos2, ou
         gate_t = keep.tile([P, 2, T], F32, name="gate_t")
         nc.sync.dma_start(out=gate_t[:], in_=gate[:, 0:P, :].rearrange("g p t -> p g t"))
 
-        x_codes = keep.tile([P, T], U32, name="x_codes", align_bytes=64)
-        for h in range(2):
-            x_bf = keep.tile([P, HALF, 4], BF16, name=f"x_bf{h}", align_bytes=64)
-            src = x_raw[h][:].rearrange("p t n -> p n t")
-            nc.vector.tensor_copy(out=x_bf[:, 0:V_COLS, :], in_=src[:, 0:V_COLS, :])
-            nc.scalar.copy(out=x_bf[:, V_COLS:HALF, :], in_=src[:, V_COLS:HALF, :])
-            cols = slice(h * HALF, (h + 1) * HALF)
-            nc.vector.quantize_mx(
-                out=x_codes[:, cols].bitcast(FP8X4),
-                scales=x_sc[:, cols],
-                in_=x_bf[:].rearrange("p n t -> p (n t)"),
-            )
+        pairs = [keep.tile([P, T, 2], BF16, name=f"pairs{u}", align_bytes=64) for u in range(2)]
+        planes = keep.tile([P, 2, T], BF16, name="planes", align_bytes=64)
+        src0 = x_raw[0][:].rearrange("p r n -> p n r")
+        nc.vector.tensor_copy(out=pairs[0][:, 0:V_COLS, :], in_=src0[:, 0:V_COLS, :])
+        nc.scalar.copy(out=pairs[0][:, V_COLS:T, :], in_=src0[:, V_COLS:T, :])
+        nc.scalar.copy(out=planes[:, 0, :], in_=x_raw[1][:, 0, :])
+        nc.scalar.copy(out=planes[:, 1, :], in_=x_raw[1][:, 1, :])
+        nc.gpsimd.tensor_copy(out=pairs[1][:], in_=x_raw[1][:].rearrange("p r n -> p n r"))
 
+        ident = keep.tile([P, P], F32, name="ident", tag="x_raw1")
+        make_identity(nc, ident[:])
+
+        s_bf = keep.tile([P, SLOTS, 4], BF16, name="s_bf", align_bytes=64)
+        s_words = s_bf[:].rearrange("p n t -> p (n t)").bitcast(U32)
         s_codes = keep.tile([P, SLOTS], U32, name="s_codes", align_bytes=64)
         s_sc = keep.tile([P, SLOTS], U8, name="s_sc", align_bytes=64)
-        banks = [[psum.tile([P, 2 * C], F32, name=f"bank{b}_{h}") for h in range(2)] for b in range(BLOCKS)]
+        slots_of = [[(0, 512, 0), (512, 768, 1), (768, 1024, 2)], [(0, 512, 2), (512, 1024, 1)], [(0, 512, 1), (512, 1024, 2)], [(0, 512, 2), (512, 1024, 1)]]
+        banks = [[(a, z, psum.tile([P, z - a], F32, name=f"bank{b}_{a}", tag=f"bank{i}")) for a, z, i in slots_of[b]] for b in range(BLOCKS)]
         y = [keep.tile([P, SLOTS], F32, name=f"y{b}") for b in range(BLOCKS)]
 
-        def gather(a, z):
-            o = offs_t[:, a // 16 : z // 16]
-            nc.vector.tensor_copy(s_codes[:, a:z], x_codes[:].indirect(o))
-            nc.vector.tensor_copy(s_sc[:, a:z], x_sc[:].indirect(o))
+        def gather(u, a, z):
+            window = pairs[u][:].rearrange("p n r -> p (n r)").bitcast(U32)
+            nc.vector.tensor_copy(s_words[:, 2 * a + u : 2 * z : 2], window.indirect(offs_t[:, a // 16 : z // 16]))
+
+        def gather_scalar(a, z):
+            for r in range(2):
+                nc.scalar.activation(s_bf[:, a:z, 2 + r], planes[:, r, :].indirect(offs_t[:, a // 16 : z // 16]), COPY)
+
+        def quantise(a, z):
+            nc.vector.quantize_mx(
+                out=s_codes[:, a:z].bitcast(FP8X4),
+                scales=s_sc[:, a:z],
+                in_=s_bf[:, a:z, :].rearrange("p n t -> p (n t)"),
+            )
 
         def multiply(b, a, z):
             e = a // C
             cols = slice(b * P, (b + 1) * P)
-            h, off = divmod(a, 2 * C)
+            lo, bank = [(lo, t) for lo, hi, t in banks[b] if lo <= a < hi][0]
             nc.tensor.matmul_mx(
-                out=banks[b][h][:, off : off + z - a],
+                out=bank[:, a - lo : z - lo],
                 lhsT=w_t[:, e, cols].bitcast(FP8X4),
                 lhsT_scale=w_sc[4 * e : P, cols],
                 rhs=s_codes[:, a:z].bitcast(FP8X4),
@@ -93,23 +105,26 @@ def tile_routed_moe_kernel(tc, xT, w_words, w_scales, gate, offs, pos1, pos2, ou
                 stop=True,
             )
 
-        gather(0, 384)
-        for b in range(BLOCKS):
-            multiply(b, 0, 256)
-            multiply(b, 256, 384)
-        gather(384, 768)
-        for b in range(BLOCKS):
-            multiply(b, 384, 512)
-            multiply(b, 512, 768)
-        nc.scalar.copy(out=y[0][:, 0:512], in_=banks[0][0][:])
-        nc.scalar.copy(out=y[0][:, 512:768], in_=banks[0][1][:, 0:256])
-        gather(768, 1024)
-        for b in range(BLOCKS):
-            multiply(b, 768, 1024)
-        nc.vector.tensor_copy(out=y[0][:, 768:1024], in_=banks[0][1][:, 256:512])
+        gather(0, 0, 384)
+        gather(0, 384, 768)
+        gather(0, 768, 1024)
+        gather_scalar(576, 768)
+        gather_scalar(768, 1024)
+        gather(1, 0, 256)
+        gather(1, 256, 576)
+        for e in range(E):
+            quantise(e * C, (e + 1) * C)
+            multiply(0, e * C, (e + 1) * C)
+            if e == 1:
+                nc.scalar.copy(out=y[0][:, 0:512], in_=banks[0][0][2][:])
+            if e == 2:
+                nc.scalar.copy(out=y[0][:, 512:768], in_=banks[0][1][2][:])
+        nc.vector.tensor_copy(out=y[0][:, 768:1024], in_=banks[0][2][2][:])
         for b in range(1, BLOCKS):
-            nc.scalar.copy(out=y[b][:, 0:512], in_=banks[b][0][:])
-            nc.scalar.copy(out=y[b][:, 512:1024], in_=banks[b][1][:])
+            for e in range(E):
+                multiply(b, e * C, (e + 1) * C)
+            nc.scalar.copy(out=y[b][:, 0:512], in_=banks[b][0][2][:])
+            nc.scalar.copy(out=y[b][:, 512:1024], in_=banks[b][1][2][:])
 
         z = [[keep.tile([P, T], F32, name=f"z{b}_{r}") for r in range(2)] for b in range(BLOCKS)]
         o_t = [keep.tile([P, T], F32, name=f"o{b}") for b in range(BLOCKS)]
@@ -122,15 +137,25 @@ def tile_routed_moe_kernel(tc, xT, w_words, w_scales, gate, offs, pos1, pos2, ou
             nc.vector.tensor_tensor(o_t[b][:, c0:c1], z[b][0][:, c0:c1], z[b][1][:, c0:c1], add)
             nc.sync.dma_start(out=out[b * P : (b + 1) * P, c0:c1], in_=o_t[b][:, c0:c1])
 
+        def finish_pe(b, bank, c0=0, c1=T):
+            acc = psum.tile([P, c1 - c0], F32, name=f"sum{b}", tag=bank)
+            nc.tensor.matmul(acc[:], ident[:], z[b][0][:, c0:c1], start=True, stop=False)
+            nc.tensor.matmul(acc[:], ident[:], z[b][1][:, c0:c1], start=False, stop=True)
+            nc.scalar.copy(out=o_t[b][:, c0:c1], in_=acc[:])
+            nc.scalar.dma_start(out=out[b * P : (b + 1) * P, c0:c1], in_=o_t[b][:, c0:c1])
+
         fetch(0, 0)
         fetch(0, 1)
-        for b in range(1, BLOCKS):
-            fetch(b, 0)
-            finish(b - 1)
-            if b < BLOCKS - 1:
-                fetch(b, 1)
-        b = BLOCKS - 1
-        fetch(b, 1, 0, 256)
-        fetch(b, 1, 256, 512)
-        finish(b, 0, 256)
-        finish(b, 256, 512)
+        fetch(1, 0)
+        finish(0)
+        fetch(1, 1)
+        finish_pe(1, "bank0")
+        fetch(2, 0)
+        fetch(2, 1)
+        finish_pe(2, "bank3", 0, 256)
+        fetch(3, 0)
+        finish(2, 256, 512)
+        fetch(3, 1, 0, 256)
+        fetch(3, 1, 256, 512)
+        finish(3, 0, 256)
+        finish(3, 256, 512)

from contextlib import ExitStack

import concourse.mybir as mybir
from concourse.masks import make_identity

K, T, E, C, N = 512, 512, 4, 256, 512
P = 128
SLOTS = E * C
BLOCKS = N // P
FLOPS = 2 * K * N * SLOTS
BYTES = 4 * K * T + E * K * N + E * K * N // 32 + 4 * 2 * T + 2 * P * (SLOTS + 2 * T) // 16 + 4 * N * T

F32 = mybir.dt.float32
BF16 = mybir.dt.bfloat16
U32 = mybir.dt.uint32
I32 = mybir.dt.int32
U16 = mybir.dt.uint16
U8 = mybir.dt.uint8
FP8X4 = mybir.dt.float8_e4m3fn_x4
mult = mybir.AluOpType.mult
COPY = mybir.ActivationFunctionType.Copy
add = mybir.AluOpType.add

V_COLS = 352


def tile_routed_moe_kernel(tc, xT, w_words, w_scales, gate, offs, pos1, pos2, out):
    nc = tc.nc
    with ExitStack() as ctx:
        keep = ctx.enter_context(tc.tile_pool(name="keep", bufs=1))
        psum = ctx.enter_context(tc.psum_pool(name="psum", bufs=1))

        x_raw = [keep.tile([P, 2, T], F32, name=f"x_raw{u}") for u in range(2)]
        x_view = xT.rearrange("(p u r) n -> u p r n", u=2, r=2)
        nc.sync.dma_start(out=x_raw[0][:, :, 0:V_COLS], in_=x_view[0][:, :, 0:V_COLS])
        nc.scalar.dma_start(out=x_raw[0][:, :, V_COLS:T], in_=x_view[0][:, :, V_COLS:T])
        offs_t = keep.tile([P, SLOTS // 16], U16, name="offs_t")
        nc.sync.dma_start(offs_t[:], offs)
        for r in range(2):
            nc.sync.dma_start(out=x_raw[1][:, r, :], in_=x_view[1][:, r, :])

        w_t = keep.tile([P, E, N], U32, name="w_t", align_bytes=64)
        w_sc = keep.tile([P, N], U8, name="w_sc", align_bytes=64)
        nc.vector.memset(w_sc[:].bitcast(I32), 0)
        for q in range(4):
            nc.sync.dma_start(
                out=w_sc[32 * q : 32 * q + 16, :].bitcast(I32),
                in_=w_scales[:, 0, 4 * q : 4 * q + 4, :].bitcast(I32),
            )
        w_view = w_words.rearrange("e a p n r -> p (e a) (n r)").bitcast(I32)
        nc.sync.dma_start(out=w_t[:, 0:2, :].bitcast(I32), in_=w_view[:, 0:2, :])
        nc.sync.dma_start(out=w_t[:, 2:4, :].bitcast(I32), in_=w_view[:, 2:4, :])
        pos_t = [keep.tile([P, T // 16], U16, name=f"pos_t{r}") for r in range(2)]
        nc.sync.dma_start(pos_t[0][:], pos1)
        nc.sync.dma_start(pos_t[1][:], pos2)
        gate_t = keep.tile([P, 2, T], F32, name="gate_t")
        nc.sync.dma_start(out=gate_t[:], in_=gate[:, 0:P, :].rearrange("g p t -> p g t"))

        pairs = [keep.tile([P, T, 2], BF16, name=f"pairs{u}", align_bytes=64) for u in range(2)]
        planes = keep.tile([P, 2, T], BF16, name="planes", align_bytes=64)
        src0 = x_raw[0][:].rearrange("p r n -> p n r")
        nc.vector.tensor_copy(out=pairs[0][:, 0:V_COLS, :], in_=src0[:, 0:V_COLS, :])
        nc.scalar.copy(out=pairs[0][:, V_COLS:T, :], in_=src0[:, V_COLS:T, :])
        nc.scalar.copy(out=planes[:, 0, :], in_=x_raw[1][:, 0, :])
        nc.scalar.copy(out=planes[:, 1, :], in_=x_raw[1][:, 1, :])
        nc.gpsimd.tensor_copy(out=pairs[1][:], in_=x_raw[1][:].rearrange("p r n -> p n r"))

        ident = keep.tile([P, P], F32, name="ident", tag="x_raw1")
        make_identity(nc, ident[:])

        s_bf = keep.tile([P, SLOTS, 4], BF16, name="s_bf", align_bytes=64)
        s_words = s_bf[:].rearrange("p n t -> p (n t)").bitcast(U32)
        s_codes = keep.tile([P, SLOTS], U32, name="s_codes", align_bytes=64)
        s_sc = keep.tile([P, SLOTS], U8, name="s_sc", align_bytes=64)
        slots_of = [[(0, 512, 0), (512, 768, 1), (768, 1024, 2)], [(0, 512, 2), (512, 1024, 1)], [(0, 512, 1), (512, 1024, 2)], [(0, 512, 2), (512, 1024, 1)]]
        banks = [[(a, z, psum.tile([P, z - a], F32, name=f"bank{b}_{a}", tag=f"bank{i}")) for a, z, i in slots_of[b]] for b in range(BLOCKS)]
        y = [keep.tile([P, SLOTS], F32, name=f"y{b}") for b in range(BLOCKS)]

        def gather(u, a, z):
            window = pairs[u][:].rearrange("p n r -> p (n r)").bitcast(U32)
            nc.vector.tensor_copy(s_words[:, 2 * a + u : 2 * z : 2], window.indirect(offs_t[:, a // 16 : z // 16]))

        def gather_scalar(a, z):
            for r in range(2):
                nc.scalar.activation(s_bf[:, a:z, 2 + r], planes[:, r, :].indirect(offs_t[:, a // 16 : z // 16]), COPY)

        def quantise(a, z):
            nc.vector.quantize_mx(
                out=s_codes[:, a:z].bitcast(FP8X4),
                scales=s_sc[:, a:z],
                in_=s_bf[:, a:z, :].rearrange("p n t -> p (n t)"),
            )

        def multiply(b, a, z):
            e = a // C
            cols = slice(b * P, (b + 1) * P)
            lo, bank = [(lo, t) for lo, hi, t in banks[b] if lo <= a < hi][0]
            nc.tensor.matmul_mx(
                out=bank[:, a - lo : z - lo],
                lhsT=w_t[:, e, cols].bitcast(FP8X4),
                lhsT_scale=w_sc[4 * e : P, cols],
                rhs=s_codes[:, a:z].bitcast(FP8X4),
                rhs_scale=s_sc[:, a:z],
                start=True,
                stop=True,
            )

        gather(0, 0, 384)
        gather(0, 384, 768)
        gather(0, 768, 1024)
        gather_scalar(576, 768)
        gather_scalar(768, 1024)
        gather(1, 0, 256)
        gather(1, 256, 576)
        for e in range(E):
            quantise(e * C, (e + 1) * C)
            multiply(0, e * C, (e + 1) * C)
            if e == 1:
                nc.scalar.copy(out=y[0][:, 0:512], in_=banks[0][0][2][:])
            if e == 2:
                nc.scalar.copy(out=y[0][:, 512:768], in_=banks[0][1][2][:])
        nc.vector.tensor_copy(out=y[0][:, 768:1024], in_=banks[0][2][2][:])
        for b in range(1, BLOCKS):
            for e in range(E):
                multiply(b, e * C, (e + 1) * C)
            nc.scalar.copy(out=y[b][:, 0:512], in_=banks[b][0][2][:])
            nc.scalar.copy(out=y[b][:, 512:1024], in_=banks[b][1][2][:])

        z = [[keep.tile([P, T], F32, name=f"z{b}_{r}") for r in range(2)] for b in range(BLOCKS)]
        o_t = [keep.tile([P, T], F32, name=f"o{b}") for b in range(BLOCKS)]

        def fetch(b, r, c0=0, c1=T):
            o = pos_t[r][:] if (c0, c1) == (0, T) else pos_t[r][:, c0 // 16 : c1 // 16]
            nc.vector.tensor_tensor(z[b][r][:, c0:c1], y[b][:].indirect(o), gate_t[:, r, c0:c1], mult)

        def finish(b, c0=0, c1=T):
            nc.vector.tensor_tensor(o_t[b][:, c0:c1], z[b][0][:, c0:c1], z[b][1][:, c0:c1], add)
            nc.sync.dma_start(out=out[b * P : (b + 1) * P, c0:c1], in_=o_t[b][:, c0:c1])

        def finish_pe(b, bank, c0=0, c1=T):
            acc = psum.tile([P, c1 - c0], F32, name=f"sum{b}", tag=bank)
            nc.tensor.matmul(acc[:], ident[:], z[b][0][:, c0:c1], start=True, stop=False)
            nc.tensor.matmul(acc[:], ident[:], z[b][1][:, c0:c1], start=False, stop=True)
            nc.scalar.copy(out=o_t[b][:, c0:c1], in_=acc[:])
            nc.scalar.dma_start(out=out[b * P : (b + 1) * P, c0:c1], in_=o_t[b][:, c0:c1])

        fetch(0, 0)
        fetch(0, 1)
        fetch(1, 0)
        finish(0)
        fetch(1, 1)
        finish_pe(1, "bank0")
        fetch(2, 0)
        fetch(2, 1)
        finish_pe(2, "bank3", 0, 256)
        fetch(3, 0)
        finish(2, 256, 512)
        fetch(3, 1, 0, 256)
        fetch(3, 1, 256, 512)
        finish(3, 0, 256)
        finish(3, 256, 512)
